import numpy as np, ml_dtypes
CORES = [2,6,10,14,18,22,26,30]
N = 8
BF = ml_dtypes.bfloat16
def gentries(a):
    return np.ascontiguousarray(a.reshape(8, 16, -1).transpose(0, 2, 1)).reshape(8, -1)
def gtable(e):
    e = np.asarray(e); return np.ascontiguousarray(e.reshape(8, -1, 16).transpose(0, 2, 1)).reshape(128, -1).astype(np.int32)
K, D, SH = 512, 2048, 3
def sized(rng):
    return rng.standard_normal((N, 128, D), dtype=np.float32) * np.exp2(rng.integers(-1, 2, (N, 128, 1))).astype(np.float32)
def hashes(a, b):
    return np.repeat(np.stack([a, b], 2), 16, axis=1).astype(np.int32)
def lists(e):
    return np.stack([gtable(u) for u in e])
def setup_inputs(rng):
    a = np.stack([rng.permutation(255)[:8] + 1 for r in range(N)]); b = rng.integers(0, 65536, (N, 8))
    return {"mat": sized(rng).astype(BF), "ids": lists(rng.integers(0, 65536, (N, 8, K))), "hs": hashes(a, b)}
def setup_inputs_ends(rng):
    e = rng.integers(0, 65536, (N, 8, K)); e = np.where(rng.random(e.shape) < 0.5, rng.choice(np.array([0, 1, 65534, 65535]), e.shape), e)
    e[:, :, 0] = 0; e[:, :, 1] = 1 << SH; e[:, :, -1] = 65535
    top = (D - 1) << SH; low = (1 << SH) - 1
    a = rng.choice(np.array([0, 1, 254, 255]), (N, 8)); b = rng.choice(np.array([0, 1, low, top, top + low, 65535]), (N, 8))
    for r in range(N):
        a[r, r % 8], b[r, r % 8] = 1, top
        a[r, (r + 1) % 8], b[r, (r + 1) % 8] = 255, 65535
        a[r, (r + 2) % 8] = 0
        a[r, (r + 3) % 8], b[r, (r + 3) % 8] = 1, top + low
    return {"mat": sized(rng).astype(BF), "ids": lists(e), "hs": hashes(a, b)}
def setup_inputs_one(rng):
    d = setup_inputs(rng); e = rng.integers(0, 65536, (N, 8, K)); o = rng.permutation(N)
    e[o[0]] = rng.permutation(65536)[:8, None]; e[o[1]] = e[o[2]]; e[o[3]] = np.repeat(e[o[3], :, :K // 16], 16, axis=1)
    d["ids"] = lists(e); d["hs"][rng.integers(0, N), :, 0] = 0; return d
def setup_inputs_turns(rng):
    d = setup_inputs(rng); p = np.argsort(rng.random((N, 8, D, 4)), axis=3)
    w = (rng.integers(128, 256, p.shape) * (2 * rng.integers(0, 2, p.shape) - 1)).astype(np.float32) * np.float32(2.0 ** -7)
    m = np.where(p[..., None] == np.arange(4), w[..., None], np.float32(0))
    d["mat"] = np.ascontiguousarray(m.transpose(0, 1, 3, 4, 2)).reshape(N, 128, D).astype(BF); return d
def setup_inputs_spread(rng):
    d = setup_inputs(rng); k = (N, 8, 1, D)
    z = (np.exp2(rng.integers(-2, 3, k)) * (rng.random(k) > 0.03125)).astype(np.float32)
    d["mat"] = (sized(rng).reshape(N, 8, 16, D) * z).reshape(N, 128, D).astype(BF); return d
def check_inputs(d):
    bad = []; h = d["hs"].reshape(N, 8, 16, 2)
    if not (np.abs(d["mat"].astype(np.float32)) <= 8192).all(): bad.append("size of mat")
    if not ((d["ids"] >= 0) & (d["ids"] <= 65535)).all(): bad.append("range of ids")
    if not ((h >= 0) & (h <= np.array([255, 65535]))).all(): bad.append("range of hs")
    if not (h == h[:, :, :1]).all(): bad.append("rows of hs alike in a group")
    return bad
def reference(mat, ids, hs):
    y = np.zeros((N, 32, K), np.float64); m = mat.astype(np.float64).reshape(N, 8, 16, D); h = hs.astype(np.int64)[:, ::16]
    for r in range(N):
        i = gentries(ids[r]).astype(np.int64)
        v = np.zeros((8, 4, K), np.float64); v[:, 0] = 1
        for q in range(N):
            t = ((i * h[q, :, :1] + h[q, :, 1:]) >> SH) & (D - 1)
            x = np.take_along_axis(m[q], t[:, None, :], 2).reshape(8, 4, 4, K)
            v = np.sum(v[:, :, None, :] * x, axis=1)
        y[r] = v.reshape(32, K)
    return {"y": y.astype(np.float32)}

@@ -1,0 +1,220 @@
+from concourse.bass import DstId, RemoteDMATransfer
+from concourse.mybir import AluOpType, ActivationFunctionType
+
+N, K, D = 8, 512, 2048
+W = K // 16
+NP = 4
+PW = K // NP
+
+SCRATCH = {
+    "idst": ("dram", [128, W], "int32"),
+    "idl": ("dram", [N, 128, W], "int32"),
+    "idsb": ("sbuf", [128, N * W], "int32"),
+    "hsi": ("sbuf", [128, 2], "int32"),
+    "hsf": ("sbuf", [128, 2], "float32"),
+    "mt": ("sbuf", [128, D], "bfloat16"),
+    "t1": ("sbuf", [128, N * W], "int32"),
+    "t2": ("sbuf", [128, N * W], "int32"),
+    "off": ("sbuf", [128, N * W], "uint16"),
+    "km": ("sbuf", [128, 128], "float32"),
+    "kf": ("sbuf", [128, 32], "float32"),
+    "pidx": ("sbuf", [128, 1], "int32"),
+    "kg": ("sbuf", [128, 1], "int32"),
+    "kc": ("sbuf", [128, 1], "int32"),
+    "am": ("sbuf", [128, 1], "int32"),
+    "key": ("sbuf", [128, 1], "float32"),
+    "a0": ("sbuf", [128, 1], "float32"),
+    "lrep": ("sbuf", [128, 128], "float32"),
+    "lsel": ("sbuf", [128, 128], "bfloat16"),
+    "lfin": ("sbuf", [128, 32], "float32"),
+    "ysb": ("sbuf", [32, K], "float32"),
+}
+for _i in range(N):
+    SCRATCH["x%d" % _i] = ("sbuf", [128, K], "bfloat16")
+for _i in range(N - 1):
+    SCRATCH["o%d" % _i] = ("sbuf", [128, K], "bfloat16")
+for _i in range(NP):
+    SCRATCH["p%d" % _i] = ("sbuf", [128, PW], "float32")
+    SCRATCH["v%d" % _i] = ("psum", [128, 512], "float32")
+
+SEMAPHORES = (["stg", "idown", "hsl", "matl", "ida", "idb", "iot", "vq", "cst", "own", "lid", "lsd", "st", "offr"]
+              + ["ia%d" % i for i in range(N)] + ["arr%d" % i for i in range(N)]
+              + ["ga%d" % i for i in range(N - 1)]
+              + ["pe%d" % i for i in range(NP)] + ["ve%d" % i for i in range(NP)] + ["yc%d" % i for i in range(NP)])
+
+
+def bits(engs):
+    m = 0
+    for e in engs:
+        m |= 1 << e
+    return m
+
+
+def peer_order(rank, core, T, topo):
+    my = topo.chip(core)
+    far, mate, plane, near = [], [], [], []
+    for r in range(N):
+        c = T.cores[r]
+        if r == rank:
+            continue
+        k = topo.chip(c)
+        if k == my:
+            near.append(r)
+        elif topo.mates(k, my):
+            mate.append(r)
+        elif topo.same_plane(k, my):
+            plane.append(r)
+        else:
+            far.append(r)
+    seq = []
+    for part in (far, mate, plane):
+        seq += sorted(part, key=lambda r: topo.die(T.cores[r]) != topo.die(core))
+    return seq[:4] + near + seq[4:]
+
+
+def rank_program(g, core, T, topo):
+    rank = T.rank_of(core)
+    if rank is None:
+        return
+    S = T.sem
+    A = AluOpType
+    peers = peer_order(rank, core, T, topo)
+    dst = [T.cores[r] for r in peers]
+    offchip = [c for c in dst if topo.chip(c) != topo.chip(core)]
+    out_engs = topo.engines(core, offchip[0])
+    home_engs = None
+    for c in dst:
+        if topo.chip(c) == topo.chip(core):
+            home_engs = [e for e in topo.engines(core, c) if e not in out_engs]
+    n_out = len(out_engs)
+
+    def arr_count(q):
+        return len(home_engs) if topo.chip(T.cores[q]) == topo.chip(core) else n_out
+
+    def blk(b):
+        return slice(b * W, (b + 1) * W)
+
+    g.sync.dma_start(T.idst[:], T.ids[:]).then_inc(S.stg, 16)
+    g.sync.dma_start(T.mt[:], T.mat[:]).then_inc(S.matl, 16)
+    g.scalar.dma_start(T.hsi[:], T.hs[:]).then_inc(S.hsl, 16)
+    g.scalar.dma_start(T.idsb[:, blk(7)], T.ids[:]).then_inc(S.idown, 16)
+    for b in range(7):
+        eng = g.sync if b % 2 == 0 else g.scalar
+        r = peers[b]
+        eng.wait_ge(S["ia%d" % r], n_out)
+        eng.dma_start(T.idsb[:, blk(b)], T.idl[r]).then_inc(S.ida if b < 2 else S.idb, 16)
+
+    g.iota(T.km[:], [[1, 32], [0, 4]], 0, 0, allow_small_or_imprecise_dtypes=True).then_inc(S.iot, 1)
+    g.iota(T.kf[:], [[1, 32]], 0, 0, allow_small_or_imprecise_dtypes=True).then_inc(S.iot, 1)
+    g.iota(T.pidx[:], [[0, 1]], 0, 1).then_inc(S.iot, 1)
+    g.wait_ge(S.stg, 16)
+    ids_dst = []
+    for c in dst:
+        rid, pid, _s = topo.addr(c)
+        ids_dst.append(DstId(rid=rid, pnc=pid))
+    g.remote_dma_fused([RemoteDMATransfer(dst_ids=ids_dst, dma_engine_mask=bits(out_engs),
+                                          remote_sem=S["ia%d" % rank], srcs=[T.idst[:]],
+                                          dsts=[T.idl[rank]] * len(dst))], local_sem=S.lid)
+    sent = 0
+    for b in range(7):
+        rid, pid, _s = topo.addr(dst[b])
+        engs = out_engs if topo.chip(dst[b]) != topo.chip(core) else home_engs
+        g.wait_ge(S["ga%d" % b], 1)
+        g.remote_dma(T["x%d" % rank][:], T["o%d" % b][:], S["arr%d" % rank], S.lsd, pid, rid, bits(engs))
+        sent += len(engs)
+    g.wait_ge(S.lid, n_out)
+    g.wait_ge(S.lsd, sent)
+
+    v = g.vector
+    n = [0]
+
+    def vop(ins):
+        ins.then_inc(S.vq, 1)
+        n[0] += 1
+
+    def vsync():
+        v.wait_ge(S.vq, n[0])
+
+    v.wait_ge(S.iot, 3)
+    vop(v.tensor_scalar(T.kg[:], T.pidx[:], 2, 28, A.arith_shift_right, A.bitwise_and))
+    vop(v.tensor_scalar(T.kc[:], T.pidx[:], 3, None, A.bitwise_and))
+    vop(v.tensor_scalar(T.am[:], T.pidx[:], 12, None, A.bitwise_and))
+    vsync()
+    vop(v.tensor_tensor(T.key[:], T.kg[:], T.kc[:], A.add))
+    vop(v.tensor_scalar(T.a0[:], T.am[:], 0.0, None, A.is_equal))
+    vsync()
+    v.tensor_scalar(T.lrep[:], T.km[:], T.key[:], None, A.is_equal).then_inc(S.cst, 1)
+    v.tensor_scalar(T.lsel[:], T.km[:], T.key[:], T.a0[:], A.is_equal, A.mult).then_inc(S.cst, 1)
+    v.tensor_scalar(T.lfin[:], T.kf[:], T.key[:], None, A.is_equal).then_inc(S.cst, 1)
+    v.wait_ge(S.hsl, 16)
+    vop(v.tensor_copy(T.hsf[:], T.hsi[:]))
+
+    def hashes(c0, c1, last):
+        vsync()
+        vop(v.tensor_scalar(T.t1[:, c0:c1], T.idsb[:, c0:c1], T.hsf[:, 0:1], T.hsf[:, 1:2], A.mult, A.add))
+        vsync()
+        vop(v.tensor_scalar(T.t2[:, c0:c1], T.t1[:, c0:c1], 3, D - 1, A.arith_shift_right, A.bitwise_and))
+        vsync()
+        v.tensor_copy(T.off[:, c0:c1], T.t2[:, c0:c1]).then_inc(S.offr, 1)
+        v.wait_ge(S.offr, last)
+
+    def pick(b):
+        return T.mt[:, 0:D].indirect(T.off[:, blk(b)])
+
+    v.wait_ge(S.idown, 16)
+    hashes(7 * W, 8 * W, 1)
+    v.wait_ge(S.matl, 16)
+    v.tensor_copy(T["x%d" % rank][:], pick(7)).then_inc(S.own, 1)
+    v.wait_ge(S.ida, 32)
+    hashes(0, 2 * W, 2)
+    v.tensor_copy(T.o0[:], pick(0)).then_inc(S.ga0, 1)
+    v.wait_ge(S.idb, 80)
+    hashes(2 * W, 7 * W, 3)
+    for b in (3, 5):
+        v.tensor_copy(T["o%d" % b][:], pick(b)).then_inc(S["ga%d" % b], 1)
+    for q in range(1, N):
+        if q == rank:
+            v.wait_ge(S.own, 1)
+        else:
+            v.wait_ge(S["arr%d" % q], arr_count(q))
+        for h in range(NP):
+            v.wait_ge(S["pe%d" % h], q)
+            v.tensor_tensor(T["p%d" % h][:], T["x%d" % q][:, h * PW:(h + 1) * PW], T["v%d" % h][:, 0:PW],
+                            A.mult).then_inc(S["ve%d" % h], 1)
+    for h in range(0, NP, 2):
+        v.wait_ge(S["pe%d" % h], N)
+        v.tensor_copy(T.ysb[:, h * PW:(h + 1) * PW], T["v%d" % h][0:32, 0:PW]).then_inc(S["yc%d" % h], 1)
+
+    t = g.tensor
+    t.wait_ge(S.cst, 3)
+    if rank == 0:
+        t.wait_ge(S.own, 1)
+    else:
+        t.wait_ge(S.arr0, arr_count(0))
+    for h in range(NP):
+        t.matmul(T["v%d" % h][:, 0:PW], T.lsel[:], T.x0[:, h * PW:(h + 1) * PW], True, True).then_inc(S["pe%d" % h], 1)
+    for q in range(1, N):
+        for h in range(NP):
+            t.wait_ge(S["ve%d" % h], q)
+            if q < N - 1:
+                t.matmul(T["v%d" % h][:, 0:PW], T.lrep[:], T["p%d" % h][:], True, True).then_inc(S["pe%d" % h], 1)
+            else:
+                t.matmul(T["v%d" % h][0:32, 0:PW], T.lfin[:], T["p%d" % h][:], True, True).then_inc(S["pe%d" % h], 1)
+
+    s = g.scalar
+    s.wait_ge(S.matl, 16)
+    s.wait_ge(S.offr, 2)
+    s.activation(T.o1[:], pick(1), ActivationFunctionType.Copy).then_inc(S.ga1, 1)
+    s.wait_ge(S.offr, 3)
+    for b in (2, 4, 6):
+        s.activation(T["o%d" % b][:], pick(b), ActivationFunctionType.Copy).then_inc(S["ga%d" % b], 1)
+    for h in range(1, NP, 2):
+        s.wait_ge(S["pe%d" % h], N)
+        s.activation(T.ysb[:, h * PW:(h + 1) * PW], T["v%d" % h][0:32, 0:PW],
+                     ActivationFunctionType.Copy).then_inc(S["yc%d" % h], 1)
+
+    for h in range(0, NP, 2):
+        g.sync.wait_ge(S["yc%d" % h], 1)
+        g.sync.wait_ge(S["yc%d" % (h + 1)], 1)
+        g.sync.dma_start(T.y[:, h * PW:(h + 2) * PW], T.ysb[:, h * PW:(h + 2) * PW]).then_inc(S.st, 16)
+    g.sync.wait_ge(S.st, 16 * (NP // 2))

@@ -5,41 +5,55 @@ N, K, D = 8, 512, 2048
 W = K // 16
 NP = 4
 PW = K // NP
+ORDER = ("mate", "far", "plane")
+JOINT = (1, 2)
 
 SCRATCH = {
-    "idst": ("dram", [128, W], "int32"),
-    "idl": ("dram", [N, 128, W], "int32"),
-    "idsb": ("sbuf", [128, N * W], "int32"),
+    "idsb": ("sbuf", [128, 4 * W], "int32"),
     "hsi": ("sbuf", [128, 2], "int32"),
-    "hsf": ("sbuf", [128, 2], "float32"),
+    "hsn": ("sbuf", [128, 2], "int32"),
+    "hf0": ("sbuf", [128, 2], "float32"),
+    "hf1": ("sbuf", [128, 2], "float32"),
     "mt": ("sbuf", [128, D], "bfloat16"),
-    "t1": ("sbuf", [128, N * W], "int32"),
-    "t2": ("sbuf", [128, N * W], "int32"),
-    "off": ("sbuf", [128, N * W], "uint16"),
+    "mn": ("sbuf", [128, D], "bfloat16"),
     "km": ("sbuf", [128, 128], "float32"),
     "kf": ("sbuf", [128, 32], "float32"),
     "pidx": ("sbuf", [128, 1], "int32"),
+    "pf": ("sbuf", [128, 1], "float32"),
     "kg": ("sbuf", [128, 1], "int32"),
     "kc": ("sbuf", [128, 1], "int32"),
     "am": ("sbuf", [128, 1], "int32"),
     "key": ("sbuf", [128, 1], "float32"),
     "a0": ("sbuf", [128, 1], "float32"),
     "lrep": ("sbuf", [128, 128], "float32"),
-    "lsel": ("sbuf", [128, 128], "bfloat16"),
     "lfin": ("sbuf", [128, 32], "float32"),
+    "wsel": ("sbuf", [128, 224], "bfloat16"),
     "ysb": ("sbuf", [32, K], "float32"),
+    "x01": ("sbuf", [128, PW + K], "bfloat16"),
 }
-for _i in range(N):
+for _i in range(2):
+    SCRATCH["ta%d" % _i] = ("sbuf", [128, 4 * W], "int32")
+    SCRATCH["tb%d" % _i] = ("sbuf", [128, 4 * W], "int32")
+    SCRATCH["off%d" % _i] = ("sbuf", [128, 4 * W], "uint16")
+    for _j in range(3):
+        SCRATCH["o%d%d" % (_i, _j)] = ("sbuf", [128, K], "bfloat16")
+for _i in range(2, N):
     SCRATCH["x%d" % _i] = ("sbuf", [128, K], "bfloat16")
-for _i in range(N - 1):
-    SCRATCH["o%d" % _i] = ("sbuf", [128, K], "bfloat16")
+for _i in range(3):
+    SCRATCH["c%d" % _i] = ("sbuf", [128, PW + K], "bfloat16")
+for _i in range(4):
+    SCRATCH["z%d" % _i] = ("sbuf", [128, K], "bfloat16")
+    SCRATCH["q%d" % _i] = ("psum", [128, 512], "float32")
 for _i in range(NP):
+    SCRATCH["ls%d" % _i] = ("sbuf", [128, 128], "bfloat16")
     SCRATCH["p%d" % _i] = ("sbuf", [128, PW], "float32")
     SCRATCH["v%d" % _i] = ("psum", [128, 512], "float32")
 
-SEMAPHORES = (["stg", "idown", "hsl", "matl", "ida", "idb", "iot", "vq", "cst", "own", "lid", "lsd", "st", "offr"]
+SEMAPHORES = (["idown", "hsl", "matl", "mna", "iot", "vq", "cst", "cls", "loc0", "loc1", "lsd", "st", "of0", "of1",
+               "hand0", "hand1"]
               + ["ia%d" % i for i in range(N)] + ["arr%d" % i for i in range(N)]
-              + ["ga%d" % i for i in range(N - 1)]
+              + ["s%d%d" % (m, i) for m in range(2) for i in range(3)]
+              + ["zr%d" % i for i in range(4)] + ["qr%d" % i for i in range(4)]
               + ["pe%d" % i for i in range(NP)] + ["ve%d" % i for i in range(NP)] + ["yc%d" % i for i in range(NP)])
 
 
@@ -50,82 +64,149 @@ def bits(engs):
     return m
 
 
-def peer_order(rank, core, T, topo):
-    my = topo.chip(core)
-    far, mate, plane, near = [], [], [], []
+def relation(a, b, topo):
+    if topo.mates(a, b):
+        return "mate"
+    return "plane" if topo.same_plane(a, b) else "far"
+
+
+def peer_order(core, T, topo):
+    found = {}
     for r in range(N):
         c = T.cores[r]
-        if r == rank:
+        if topo.chip(c) != topo.chip(core) and topo.die(c) == topo.die(core):
+            found[relation(topo.chip(core), topo.chip(c), topo)] = r
+    return [found[k] for k in ORDER]
+
+
+def modes_of(core, T, topo):
+    rank = T.rank_of(core)
+    return [rank] + [r for r in range(N) if r != rank and topo.chip(T.cores[r]) == topo.chip(core)]
+
+
+def helper_of(core, T, topo):
+    to = T.cores[peer_order(core, T, topo)[0]]
+    for h in topo.cores_of(core):
+        if T.rank_of(h) is None and topo.die(h) == topo.die(core) and topo.may_write(h, to):
+            return h
+
+
+def hand_engines(core, m, T, topo):
+    modes = modes_of(core, T, topo)
+    to = T.cores[peer_order(core, T, topo)[0]]
+    out = topo.engines(core, to)
+    every = topo.engines(core, helper_of(core, T, topo))
+    if m == 1 and modes[1] == 0:
+        return []
+    if m == 1 and modes[0] == 0:
+        return every
+    return [e for e in every if e not in out]
+
+
+def landing(T, q):
+    if q == 0:
+        return T.x01[:, 0:PW]
+    return T.x01[:, PW:PW + K] if q == 1 else T["x%d" % q][:]
+
+
+def outgoing(T, m, q, b):
+    if q == 0:
+        return T["c%d" % b][:, 0:PW]
+    return T["c%d" % b][:, PW:PW + K] if q == 1 else T["o%d%d" % (m, b)][:]
+
+
+def relay(g, core, T, topo):
+    S = T.sem
+    for c in T.cores:
+        if helper_of(c, T, topo) != core:
             continue
-        k = topo.chip(c)
-        if k == my:
-            near.append(r)
-        elif topo.mates(k, my):
-            mate.append(r)
-        elif topo.same_plane(k, my):
-            plane.append(r)
-        else:
-            far.append(r)
-    seq = []
-    for part in (far, mate, plane):
-        seq += sorted(part, key=lambda r: topo.die(T.cores[r]) != topo.die(core))
-    return seq[:4] + near + seq[4:]
+        to = T.cores[peer_order(c, T, topo)[0]]
+        rid, pid, _s = topo.addr(to)
+        engs = topo.engines(core, to)
+        sent = 0
+        for m, q in enumerate(modes_of(c, T, topo)):
+            hand = hand_engines(c, m, T, topo)
+            if hand:
+                g.wait_ge(S["hand%d" % m], len(hand))
+                g.remote_dma(landing(T, q), outgoing(T, m, q, 0), S["arr%d" % q], S.lsd, pid, rid, bits(engs))
+                sent += len(engs)
+        g.wait_ge(S.lsd, sent)
 
 
 def rank_program(g, core, T, topo):
     rank = T.rank_of(core)
     if rank is None:
+        relay(g, core, T, topo)
         return
     S = T.sem
     A = AluOpType
-    peers = peer_order(rank, core, T, topo)
-    dst = [T.cores[r] for r in peers]
-    offchip = [c for c in dst if topo.chip(c) != topo.chip(core)]
-    out_engs = topo.engines(core, offchip[0])
-    home_engs = None
-    for c in dst:
-        if topo.chip(c) == topo.chip(core):
-            home_engs = [e for e in topo.engines(core, c) if e not in out_engs]
+    COPY = ActivationFunctionType.Copy
+    mode = modes_of(core, T, topo)
+    near = mode[1]
+    peers = peer_order(core, T, topo)
+    out_engs = topo.engines(core, T.cores[peers[0]])
+    all_engs = topo.engines(core, T.cores[near])
+    home_engs = [e for e in all_engs if e not in out_engs]
     n_out = len(out_engs)
-
-    def arr_count(q):
-        return len(home_engs) if topo.chip(T.cores[q]) == topo.chip(core) else n_out
+    first = 0 in mode
+    lead = mode[0] == 0
+    joint = JOINT if lead else ()
+    joint_in = 0 in peers and peers.index(0) in JOINT
 
     def blk(b):
         return slice(b * W, (b + 1) * W)
 
-    g.sync.dma_start(T.idst[:], T.ids[:]).then_inc(S.stg, 16)
+    def x(q):
+        return landing(T, q)
+
+    def o(m, b):
+        return outgoing(T, m, mode[m], b)
+
+    g.sync.dma_start(T.idsb[:, blk(3)], T.ids[:]).then_inc(S.idown, 16)
     g.sync.dma_start(T.mt[:], T.mat[:]).then_inc(S.matl, 16)
     g.scalar.dma_start(T.hsi[:], T.hs[:]).then_inc(S.hsl, 16)
-    g.scalar.dma_start(T.idsb[:, blk(7)], T.ids[:]).then_inc(S.idown, 16)
-    for b in range(7):
-        eng = g.sync if b % 2 == 0 else g.scalar
-        r = peers[b]
-        eng.wait_ge(S["ia%d" % r], n_out)
-        eng.dma_start(T.idsb[:, blk(b)], T.idl[r]).then_inc(S.ida if b < 2 else S.idb, 16)
 
     g.iota(T.km[:], [[1, 32], [0, 4]], 0, 0, allow_small_or_imprecise_dtypes=True).then_inc(S.iot, 1)
     g.iota(T.kf[:], [[1, 32]], 0, 0, allow_small_or_imprecise_dtypes=True).then_inc(S.iot, 1)
     g.iota(T.pidx[:], [[0, 1]], 0, 1).then_inc(S.iot, 1)
-    g.wait_ge(S.stg, 16)
+    g.wait_ge(S.idown, 16)
     ids_dst = []
-    for c in dst:
-        rid, pid, _s = topo.addr(c)
+    for r in peers:
+        rid, pid, _s = topo.addr(T.cores[r])
         ids_dst.append(DstId(rid=rid, pnc=pid))
-    g.remote_dma_fused([RemoteDMATransfer(dst_ids=ids_dst, dma_engine_mask=bits(out_engs),
-                                          remote_sem=S["ia%d" % rank], srcs=[T.idst[:]],
-                                          dsts=[T.idl[rank]] * len(dst))], local_sem=S.lid)
-    sent = 0
-    for b in range(7):
-        rid, pid, _s = topo.addr(dst[b])
-        engs = out_engs if topo.chip(dst[b]) != topo.chip(core) else home_engs
-        g.wait_ge(S["ga%d" % b], 1)
-        g.remote_dma(T["x%d" % rank][:], T["o%d" % b][:], S["arr%d" % rank], S.lsd, pid, rid, bits(engs))
-        sent += len(engs)
-    g.wait_ge(S.lid, n_out)
+    g.remote_dma_fused([RemoteDMATransfer(dst_ids=ids_dst, dma_engine_mask=bits(out_engs), remote_sem=S["ia%d" % rank],
+                                          srcs=[T.idsb[:, blk(3)]], dsts=[T.idsb[:, blk(b)] for b in range(3)])],
+                       local_sem=S.lsd)
+    nrid, npid, _s = topo.addr(T.cores[near])
+    g.wait_ge(S.hsl, 16)
+    g.remote_dma(T.hsn[:], T.hsi[:], S["ia%d" % rank], S.lsd, npid, nrid, bits(home_engs))
+    g.wait_ge(S.matl, 16)
+    g.remote_dma(T.mn[:], T.mt[:], S.mna, S.lsd, npid, nrid, bits(all_engs))
+    sent = n_out + len(home_engs) + len(all_engs)
+    for m in range(2):
+        hand = hand_engines(core, m, T, topo)
+        for b in range(3):
+            if b in joint and m == 0:
+                continue
+            if b in joint:
+                g.wait_ge(S["s0%d" % b], 1)
+            g.wait_ge(S["s%d%d" % (m, b)], 1)
+            if b == 0 and hand:
+                rid, pid, _s = topo.addr(helper_of(core, T, topo))
+                g.remote_dma(o(m, b), o(m, b), S["hand%d" % m], S.lsd, pid, rid, bits(hand))
+                sent += len(hand)
+                continue
+            rid, pid, _s = topo.addr(T.cores[peers[b]])
+            if b in joint:
+                g.remote_dma(T.x01[:], T["c%d" % b][:], S.arr1, S.lsd, pid, rid, bits(out_engs))
+            else:
+                g.remote_dma(x(mode[m]), o(m, b), S["arr%d" % mode[m]], S.lsd, pid, rid, bits(out_engs))
+            sent += n_out
     g.wait_ge(S.lsd, sent)
 
     v = g.vector
+    s = g.scalar
+    t = g.tensor
     n = [0]
 
     def vop(ins):
@@ -139,60 +220,139 @@ def rank_program(g, core, T, topo):
     vop(v.tensor_scalar(T.kg[:], T.pidx[:], 2, 28, A.arith_shift_right, A.bitwise_and))
     vop(v.tensor_scalar(T.kc[:], T.pidx[:], 3, None, A.bitwise_and))
     vop(v.tensor_scalar(T.am[:], T.pidx[:], 12, None, A.bitwise_and))
+    vop(v.tensor_copy(T.pf[:], T.pidx[:]))
+    if first:
+        vop(v.memset(T.wsel[:], 0.0))
     vsync()
     vop(v.tensor_tensor(T.key[:], T.kg[:], T.kc[:], A.add))
     vop(v.tensor_scalar(T.a0[:], T.am[:], 0.0, None, A.is_equal))
     vsync()
+    ncst = 2
+    if first:
+        v.tensor_scalar(T.wsel[:, 96:128], T.kf[:], T.key[:], T.a0[:], A.is_equal, A.mult).then_inc(S.cst, 1)
+        ncst += 1
     v.tensor_scalar(T.lrep[:], T.km[:], T.key[:], None, A.is_equal).then_inc(S.cst, 1)
-    v.tensor_scalar(T.lsel[:], T.km[:], T.key[:], T.a0[:], A.is_equal, A.mult).then_inc(S.cst, 1)
     v.tensor_scalar(T.lfin[:], T.kf[:], T.key[:], None, A.is_equal).then_inc(S.cst, 1)
-    v.wait_ge(S.hsl, 16)
-    vop(v.tensor_copy(T.hsf[:], T.hsi[:]))
 
-    def hashes(c0, c1, last):
-        vsync()
-        vop(v.tensor_scalar(T.t1[:, c0:c1], T.idsb[:, c0:c1], T.hsf[:, 0:1], T.hsf[:, 1:2], A.mult, A.add))
-        vsync()
-        vop(v.tensor_scalar(T.t2[:, c0:c1], T.t1[:, c0:c1], 3, D - 1, A.arith_shift_right, A.bitwise_and))
-        vsync()
-        v.tensor_copy(T.off[:, c0:c1], T.t2[:, c0:c1]).then_inc(S.offr, 1)
-        v.wait_ge(S.offr, last)
+    def lsels():
+        for h in range(NP):
+            v.tensor_scalar(T["ls%d" % h][:], T.km[:], 32.0 * h, T.pf[:], A.add, A.is_equal).then_inc(S.cls, 1)
 
-    def pick(b):
-        return T.mt[:, 0:D].indirect(T.off[:, blk(b)])
+    def hashes(m, b0, b1):
+        c0, c1 = b0 * W, b1 * W
+        ta, tb, off, hf = T["ta%d" % m], T["tb%d" % m], T["off%d" % m], T["hf%d" % m]
+        vsync()
+        vop(v.tensor_scalar(ta[:, c0:c1], T.idsb[:, c0:c1], hf[:, 0:1], hf[:, 1:2], A.mult, A.add))
+        vsync()
+        vop(v.tensor_scalar(tb[:, c0:c1], ta[:, c0:c1], 3, D - 1, A.arith_shift_right, A.bitwise_and))
+        vsync()
+        v.tensor_copy(off[:, c0:c1], tb[:, c0:c1]).then_inc(S["of%d" % m], 1)
 
-    v.wait_ge(S.idown, 16)
-    hashes(7 * W, 8 * W, 1)
-    v.wait_ge(S.matl, 16)
-    v.tensor_copy(T["x%d" % rank][:], pick(7)).then_inc(S.own, 1)
-    v.wait_ge(S.ida, 32)
-    hashes(0, 2 * W, 2)
-    v.tensor_copy(T.o0[:], pick(0)).then_inc(S.ga0, 1)
-    v.wait_ge(S.idb, 80)
-    hashes(2 * W, 7 * W, 3)
-    for b in (3, 5):
-        v.tensor_copy(T["o%d" % b][:], pick(b)).then_inc(S["ga%d" % b], 1)
-    for q in range(1, N):
-        if q == rank:
-            v.wait_ge(S.own, 1)
+    def near_hashes():
+        v.wait_ge(S["ia%d" % near], len(home_engs))
+        vop(v.tensor_copy(T.hf1[:], T.hsn[:]))
+        hashes(1, 0, 4)
+
+    def gather(q, m, b):
+        q.wait_ge(S["of%d" % m], 1 if m == 1 or b == 3 else (2 if b == 0 else 3))
+        if m == 0:
+            q.wait_ge(S.matl, 16)
         else:
-            v.wait_ge(S["arr%d" % q], arr_count(q))
+            q.wait_ge(S.mna, len(all_engs))
+        if mode[m] == 0:
+            out, sem = T["z%d" % b][:], S["zr%d" % b]
+        elif b == 3:
+            out, sem = x(mode[m]), S["loc%d" % m]
+        else:
+            out, sem = o(m, b), S["s%d%d" % (m, b)]
+        win = (T.mt if m == 0 else T.mn)[:, 0:D].indirect(T["off%d" % m][:, blk(b)])
+        if q is v:
+            v.tensor_copy(out, win).then_inc(sem, 1)
+        else:
+            s.activation(out, win, COPY).then_inc(sem, 1)
+
+    def squeeze(b):
+        t.wait_ge(S["zr%d" % b], 1)
+        for h in range(4):
+            ins = t.matmul(T["q%d" % b][:, 0:PW], T.wsel[:, 96 - 32 * h:224 - 32 * h],
+                           T["z%d" % b][:, h * PW:(h + 1) * PW], h == 0, h == 3)
+        ins.then_inc(S["qr%d" % b], 1)
+
+    def unload(q, b):
+        m = mode.index(0)
+        out, sem = (x(0), S["loc%d" % m]) if b == 3 else (o(m, b), S["s%d%d" % (m, b)])
+        q.wait_ge(S["qr%d" % b], 1)
+        if q is v:
+            v.tensor_copy(out, T["q%d" % b][:, 0:PW]).then_inc(sem, 1)
+        else:
+            s.activation(out, T["q%d" % b][:, 0:PW], COPY).then_inc(sem, 1)
+
+    v.wait_ge(S.hsl, 16)
+    vop(v.tensor_copy(T.hf0[:], T.hsi[:]))
+    v.wait_ge(S.idown, 16)
+    hashes(0, 3, 4)
+    v.wait_ge(S["ia%d" % peers[0]], n_out)
+    hashes(0, 0, 1)
+    for b in (1, 2):
+        v.wait_ge(S["ia%d" % peers[b]], n_out)
+    hashes(0, 1, 3)
+    if lead:
+        near_hashes()
+        gather(v, 0, 1)
+        gather(v, 1, 0)
+        unload(v, 1)
+        gather(v, 1, 2)
+    else:
+        gather(v, 0, 1)
+        near_hashes()
+        gather(v, 1, 1)
+        gather(v, 1, 2)
+        if first:
+            unload(v, 2)
+    lsels()
+
+    gather(s, 0, 3)
+    gather(s, 0, 0)
+    if lead:
+        unload(s, 0)
+        gather(s, 0, 2)
+        gather(s, 1, 1)
+        unload(s, 2)
+    else:
+        gather(s, 0, 2)
+        gather(s, 1, 0)
+        if first:
+            unload(s, 0)
+            unload(s, 1)
+    gather(s, 1, 3)
+    if first:
+        unload(s, 3)
+
+    t.wait_ge(S.cst, ncst)
+    if first:
+        for b in ((3, 0, 1, 2) if lead else (0, 1, 2, 3)):
+            squeeze(b)
+
+    def ready(q, m):
+        if m in mode:
+            q.wait_ge(S["loc%d" % mode.index(m)], 1)
+        else:
+            q.wait_ge(S.arr1 if m == 0 and joint_in else S["arr%d" % m], n_out)
+
+    for q in range(1, N):
+        ready(v, q)
         for h in range(NP):
             v.wait_ge(S["pe%d" % h], q)
-            v.tensor_tensor(T["p%d" % h][:], T["x%d" % q][:, h * PW:(h + 1) * PW], T["v%d" % h][:, 0:PW],
+            v.tensor_tensor(T["p%d" % h][:], x(q)[:, h * PW:(h + 1) * PW], T["v%d" % h][:, 0:PW],
                             A.mult).then_inc(S["ve%d" % h], 1)
-    for h in range(0, NP, 2):
+    for h in range(1, NP, 2):
         v.wait_ge(S["pe%d" % h], N)
         v.tensor_copy(T.ysb[:, h * PW:(h + 1) * PW], T["v%d" % h][0:32, 0:PW]).then_inc(S["yc%d" % h], 1)
 
-    t = g.tensor
-    t.wait_ge(S.cst, 3)
-    if rank == 0:
-        t.wait_ge(S.own, 1)
-    else:
-        t.wait_ge(S.arr0, arr_count(0))
+    t.wait_ge(S.cls, NP)
+    ready(t, 0)
     for h in range(NP):
-        t.matmul(T["v%d" % h][:, 0:PW], T.lsel[:], T.x0[:, h * PW:(h + 1) * PW], True, True).then_inc(S["pe%d" % h], 1)
+        t.matmul(T["v%d" % h][:, 0:PW], T["ls%d" % h][:], x(0), True, True).then_inc(S["pe%d" % h], 1)
     for q in range(1, N):
         for h in range(NP):
             t.wait_ge(S["ve%d" % h], q)
@@ -201,17 +361,9 @@ def rank_program(g, core, T, topo):
             else:
                 t.matmul(T["v%d" % h][0:32, 0:PW], T.lfin[:], T["p%d" % h][:], True, True).then_inc(S["pe%d" % h], 1)
 
-    s = g.scalar
-    s.wait_ge(S.matl, 16)
-    s.wait_ge(S.offr, 2)
-    s.activation(T.o1[:], pick(1), ActivationFunctionType.Copy).then_inc(S.ga1, 1)
-    s.wait_ge(S.offr, 3)
-    for b in (2, 4, 6):
-        s.activation(T["o%d" % b][:], pick(b), ActivationFunctionType.Copy).then_inc(S["ga%d" % b], 1)
-    for h in range(1, NP, 2):
+    for h in range(0, NP, 2):
         s.wait_ge(S["pe%d" % h], N)
-        s.activation(T.ysb[:, h * PW:(h + 1) * PW], T["v%d" % h][0:32, 0:PW],
-                     ActivationFunctionType.Copy).then_inc(S["yc%d" % h], 1)
+        s.activation(T.ysb[:, h * PW:(h + 1) * PW], T["v%d" % h][0:32, 0:PW], COPY).then_inc(S["yc%d" % h], 1)
 
     for h in range(0, NP, 2):
         g.sync.wait_ge(S["yc%d" % h], 1)

from concourse.bass import DstId, RemoteDMATransfer
from concourse.mybir import AluOpType, ActivationFunctionType

N, K, D = 8, 512, 2048
W = K // 16
NP = 4
PW = K // NP
ORDER = ("mate", "far", "plane")
JOINT = (1, 2)

SCRATCH = {
    "idsb": ("sbuf", [128, 4 * W], "int32"),
    "hsi": ("sbuf", [128, 2], "int32"),
    "hsn": ("sbuf", [128, 2], "int32"),
    "hf0": ("sbuf", [128, 2], "float32"),
    "hf1": ("sbuf", [128, 2], "float32"),
    "mt": ("sbuf", [128, D], "bfloat16"),
    "mn": ("sbuf", [128, D], "bfloat16"),
    "km": ("sbuf", [128, 128], "float32"),
    "kf": ("sbuf", [128, 32], "float32"),
    "pidx": ("sbuf", [128, 1], "int32"),
    "pf": ("sbuf", [128, 1], "float32"),
    "kg": ("sbuf", [128, 1], "int32"),
    "kc": ("sbuf", [128, 1], "int32"),
    "am": ("sbuf", [128, 1], "int32"),
    "key": ("sbuf", [128, 1], "float32"),
    "a0": ("sbuf", [128, 1], "float32"),
    "lrep": ("sbuf", [128, 128], "float32"),
    "lfin": ("sbuf", [128, 32], "float32"),
    "wsel": ("sbuf", [128, 224], "bfloat16"),
    "ysb": ("sbuf", [32, K], "float32"),
    "x01": ("sbuf", [128, PW + K], "bfloat16"),
}
for _i in range(2):
    SCRATCH["ta%d" % _i] = ("sbuf", [128, 4 * W], "int32")
    SCRATCH["tb%d" % _i] = ("sbuf", [128, 4 * W], "int32")
    SCRATCH["off%d" % _i] = ("sbuf", [128, 4 * W], "uint16")
    for _j in range(3):
        SCRATCH["o%d%d" % (_i, _j)] = ("sbuf", [128, K], "bfloat16")
for _i in range(2, N):
    SCRATCH["x%d" % _i] = ("sbuf", [128, K], "bfloat16")
for _i in range(3):
    SCRATCH["c%d" % _i] = ("sbuf", [128, PW + K], "bfloat16")
for _i in range(4):
    SCRATCH["z%d" % _i] = ("sbuf", [128, K], "bfloat16")
    SCRATCH["q%d" % _i] = ("psum", [128, 512], "float32")
for _i in range(NP):
    SCRATCH["ls%d" % _i] = ("sbuf", [128, 128], "bfloat16")
    SCRATCH["p%d" % _i] = ("sbuf", [128, PW], "float32")
    SCRATCH["v%d" % _i] = ("psum", [128, 512], "float32")

SEMAPHORES = (["idown", "hsl", "matl", "mna", "iot", "vq", "cst", "cls", "loc0", "loc1", "lsd", "st", "of0", "of1",
               "hand0", "hand1"]
              + ["ia%d" % i for i in range(N)] + ["arr%d" % i for i in range(N)]
              + ["s%d%d" % (m, i) for m in range(2) for i in range(3)]
              + ["zr%d" % i for i in range(4)] + ["qr%d" % i for i in range(4)]
              + ["pe%d" % i for i in range(NP)] + ["ve%d" % i for i in range(NP)] + ["yc%d" % i for i in range(NP)])


def bits(engs):
    m = 0
    for e in engs:
        m |= 1 << e
    return m


def relation(a, b, topo):
    if topo.mates(a, b):
        return "mate"
    return "plane" if topo.same_plane(a, b) else "far"


def peer_order(core, T, topo):
    found = {}
    for r in range(N):
        c = T.cores[r]
        if topo.chip(c) != topo.chip(core) and topo.die(c) == topo.die(core):
            found[relation(topo.chip(core), topo.chip(c), topo)] = r
    return [found[k] for k in ORDER]


def modes_of(core, T, topo):
    rank = T.rank_of(core)
    return [rank] + [r for r in range(N) if r != rank and topo.chip(T.cores[r]) == topo.chip(core)]


def helper_of(core, T, topo):
    to = T.cores[peer_order(core, T, topo)[0]]
    for h in topo.cores_of(core):
        if T.rank_of(h) is None and topo.die(h) == topo.die(core) and topo.may_write(h, to):
            return h


def hand_engines(core, m, T, topo):
    modes = modes_of(core, T, topo)
    to = T.cores[peer_order(core, T, topo)[0]]
    out = topo.engines(core, to)
    every = topo.engines(core, helper_of(core, T, topo))
    if m == 1 and modes[1] == 0:
        return []
    if m == 1 and modes[0] == 0:
        return every
    return [e for e in every if e not in out]


def landing(T, q):
    if q == 0:
        return T.x01[:, 0:PW]
    return T.x01[:, PW:PW + K] if q == 1 else T["x%d" % q][:]


def outgoing(T, m, q, b):
    if q == 0:
        return T["c%d" % b][:, 0:PW]
    return T["c%d" % b][:, PW:PW + K] if q == 1 else T["o%d%d" % (m, b)][:]


def relay(g, core, T, topo):
    S = T.sem
    for c in T.cores:
        if helper_of(c, T, topo) != core:
            continue
        to = T.cores[peer_order(c, T, topo)[0]]
        rid, pid, _s = topo.addr(to)
        engs = topo.engines(core, to)
        sent = 0
        for m, q in enumerate(modes_of(c, T, topo)):
            hand = hand_engines(c, m, T, topo)
            if hand:
                g.wait_ge(S["hand%d" % m], len(hand))
                g.remote_dma(landing(T, q), outgoing(T, m, q, 0), S["arr%d" % q], S.lsd, pid, rid, bits(engs))
                sent += len(engs)
        g.wait_ge(S.lsd, sent)


def rank_program(g, core, T, topo):
    rank = T.rank_of(core)
    if rank is None:
        relay(g, core, T, topo)
        return
    S = T.sem
    A = AluOpType
    COPY = ActivationFunctionType.Copy
    mode = modes_of(core, T, topo)
    near = mode[1]
    peers = peer_order(core, T, topo)
    out_engs = topo.engines(core, T.cores[peers[0]])
    all_engs = topo.engines(core, T.cores[near])
    home_engs = [e for e in all_engs if e not in out_engs]
    n_out = len(out_engs)
    first = 0 in mode
    lead = mode[0] == 0
    joint = JOINT if lead else ()
    joint_in = 0 in peers and peers.index(0) in JOINT

    def blk(b):
        return slice(b * W, (b + 1) * W)

    def x(q):
        return landing(T, q)

    def o(m, b):
        return outgoing(T, m, mode[m], b)

    g.sync.dma_start(T.idsb[:, blk(3)], T.ids[:]).then_inc(S.idown, 16)
    g.sync.dma_start(T.mt[:], T.mat[:]).then_inc(S.matl, 16)
    g.scalar.dma_start(T.hsi[:], T.hs[:]).then_inc(S.hsl, 16)

    g.iota(T.km[:], [[1, 32], [0, 4]], 0, 0, allow_small_or_imprecise_dtypes=True).then_inc(S.iot, 1)
    g.iota(T.kf[:], [[1, 32]], 0, 0, allow_small_or_imprecise_dtypes=True).then_inc(S.iot, 1)
    g.iota(T.pidx[:], [[0, 1]], 0, 1).then_inc(S.iot, 1)
    g.wait_ge(S.idown, 16)
    ids_dst = []
    for r in peers:
        rid, pid, _s = topo.addr(T.cores[r])
        ids_dst.append(DstId(rid=rid, pnc=pid))
    g.remote_dma_fused([RemoteDMATransfer(dst_ids=ids_dst, dma_engine_mask=bits(out_engs), remote_sem=S["ia%d" % rank],
                                          srcs=[T.idsb[:, blk(3)]], dsts=[T.idsb[:, blk(b)] for b in range(3)])],
                       local_sem=S.lsd)
    nrid, npid, _s = topo.addr(T.cores[near])
    g.wait_ge(S.hsl, 16)
    g.remote_dma(T.hsn[:], T.hsi[:], S["ia%d" % rank], S.lsd, npid, nrid, bits(home_engs))
    g.wait_ge(S.matl, 16)
    g.remote_dma(T.mn[:], T.mt[:], S.mna, S.lsd, npid, nrid, bits(all_engs))
    sent = n_out + len(home_engs) + len(all_engs)
    for m in range(2):
        hand = hand_engines(core, m, T, topo)
        for b in range(3):
            if b in joint and m == 0:
                continue
            if b in joint:
                g.wait_ge(S["s0%d" % b], 1)
            g.wait_ge(S["s%d%d" % (m, b)], 1)
            if b == 0 and hand:
                rid, pid, _s = topo.addr(helper_of(core, T, topo))
                g.remote_dma(o(m, b), o(m, b), S["hand%d" % m], S.lsd, pid, rid, bits(hand))
                sent += len(hand)
                continue
            rid, pid, _s = topo.addr(T.cores[peers[b]])
            if b in joint:
                g.remote_dma(T.x01[:], T["c%d" % b][:], S.arr1, S.lsd, pid, rid, bits(out_engs))
            else:
                g.remote_dma(x(mode[m]), o(m, b), S["arr%d" % mode[m]], S.lsd, pid, rid, bits(out_engs))
            sent += n_out
    g.wait_ge(S.lsd, sent)

    v = g.vector
    s = g.scalar
    t = g.tensor
    n = [0]

    def vop(ins):
        ins.then_inc(S.vq, 1)
        n[0] += 1

    def vsync():
        v.wait_ge(S.vq, n[0])

    v.wait_ge(S.iot, 3)
    vop(v.tensor_scalar(T.kg[:], T.pidx[:], 2, 28, A.arith_shift_right, A.bitwise_and))
    vop(v.tensor_scalar(T.kc[:], T.pidx[:], 3, None, A.bitwise_and))
    vop(v.tensor_scalar(T.am[:], T.pidx[:], 12, None, A.bitwise_and))
    vop(v.tensor_copy(T.pf[:], T.pidx[:]))
    if first:
        vop(v.memset(T.wsel[:], 0.0))
    vsync()
    vop(v.tensor_tensor(T.key[:], T.kg[:], T.kc[:], A.add))
    vop(v.tensor_scalar(T.a0[:], T.am[:], 0.0, None, A.is_equal))
    vsync()
    ncst = 2
    if first:
        v.tensor_scalar(T.wsel[:, 96:128], T.kf[:], T.key[:], T.a0[:], A.is_equal, A.mult).then_inc(S.cst, 1)
        ncst += 1
    v.tensor_scalar(T.lrep[:], T.km[:], T.key[:], None, A.is_equal).then_inc(S.cst, 1)
    v.tensor_scalar(T.lfin[:], T.kf[:], T.key[:], None, A.is_equal).then_inc(S.cst, 1)

    def lsels():
        for h in range(NP):
            v.tensor_scalar(T["ls%d" % h][:], T.km[:], 32.0 * h, T.pf[:], A.add, A.is_equal).then_inc(S.cls, 1)

    def hashes(m, b0, b1):
        c0, c1 = b0 * W, b1 * W
        ta, tb, off, hf = T["ta%d" % m], T["tb%d" % m], T["off%d" % m], T["hf%d" % m]
        vsync()
        vop(v.tensor_scalar(ta[:, c0:c1], T.idsb[:, c0:c1], hf[:, 0:1], hf[:, 1:2], A.mult, A.add))
        vsync()
        vop(v.tensor_scalar(tb[:, c0:c1], ta[:, c0:c1], 3, D - 1, A.arith_shift_right, A.bitwise_and))
        vsync()
        v.tensor_copy(off[:, c0:c1], tb[:, c0:c1]).then_inc(S["of%d" % m], 1)

    def near_hashes():
        v.wait_ge(S["ia%d" % near], len(home_engs))
        vop(v.tensor_copy(T.hf1[:], T.hsn[:]))
        hashes(1, 0, 4)

    def gather(q, m, b):
        q.wait_ge(S["of%d" % m], 1 if m == 1 or b == 3 else (2 if b == 0 else 3))
        if m == 0:
            q.wait_ge(S.matl, 16)
        else:
            q.wait_ge(S.mna, len(all_engs))
        if mode[m] == 0:
            out, sem = T["z%d" % b][:], S["zr%d" % b]
        elif b == 3:
            out, sem = x(mode[m]), S["loc%d" % m]
        else:
            out, sem = o(m, b), S["s%d%d" % (m, b)]
        win = (T.mt if m == 0 else T.mn)[:, 0:D].indirect(T["off%d" % m][:, blk(b)])
        if q is v:
            v.tensor_copy(out, win).then_inc(sem, 1)
        else:
            s.activation(out, win, COPY).then_inc(sem, 1)

    def squeeze(b):
        t.wait_ge(S["zr%d" % b], 1)
        for h in range(4):
            ins = t.matmul(T["q%d" % b][:, 0:PW], T.wsel[:, 96 - 32 * h:224 - 32 * h],
                           T["z%d" % b][:, h * PW:(h + 1) * PW], h == 0, h == 3)
        ins.then_inc(S["qr%d" % b], 1)

    def unload(q, b):
        m = mode.index(0)
        out, sem = (x(0), S["loc%d" % m]) if b == 3 else (o(m, b), S["s%d%d" % (m, b)])
        q.wait_ge(S["qr%d" % b], 1)
        if q is v:
            v.tensor_copy(out, T["q%d" % b][:, 0:PW]).then_inc(sem, 1)
        else:
            s.activation(out, T["q%d" % b][:, 0:PW], COPY).then_inc(sem, 1)

    v.wait_ge(S.hsl, 16)
    vop(v.tensor_copy(T.hf0[:], T.hsi[:]))
    v.wait_ge(S.idown, 16)
    hashes(0, 3, 4)
    v.wait_ge(S["ia%d" % peers[0]], n_out)
    hashes(0, 0, 1)
    for b in (1, 2):
        v.wait_ge(S["ia%d" % peers[b]], n_out)
    hashes(0, 1, 3)
    if lead:
        near_hashes()
        gather(v, 0, 1)
        gather(v, 1, 0)
        unload(v, 1)
        gather(v, 1, 2)
    else:
        gather(v, 0, 1)
        near_hashes()
        gather(v, 1, 1)
        gather(v, 1, 2)
        if first:
            unload(v, 2)
    lsels()

    gather(s, 0, 3)
    gather(s, 0, 0)
    if lead:
        unload(s, 0)
        gather(s, 0, 2)
        gather(s, 1, 1)
        unload(s, 2)
    else:
        gather(s, 0, 2)
        gather(s, 1, 0)
        if first:
            unload(s, 0)
            unload(s, 1)
    gather(s, 1, 3)
    if first:
        unload(s, 3)

    t.wait_ge(S.cst, ncst)
    if first:
        for b in ((3, 0, 1, 2) if lead else (0, 1, 2, 3)):
            squeeze(b)

    def ready(q, m):
        if m in mode:
            q.wait_ge(S["loc%d" % mode.index(m)], 1)
        else:
            q.wait_ge(S.arr1 if m == 0 and joint_in else S["arr%d" % m], n_out)

    for q in range(1, N):
        ready(v, q)
        for h in range(NP):
            v.wait_ge(S["pe%d" % h], q)
            v.tensor_tensor(T["p%d" % h][:], x(q)[:, h * PW:(h + 1) * PW], T["v%d" % h][:, 0:PW],
                            A.mult).then_inc(S["ve%d" % h], 1)
    for h in range(1, NP, 2):
        v.wait_ge(S["pe%d" % h], N)
        v.tensor_copy(T.ysb[:, h * PW:(h + 1) * PW], T["v%d" % h][0:32, 0:PW]).then_inc(S["yc%d" % h], 1)

    t.wait_ge(S.cls, NP)
    ready(t, 0)
    for h in range(NP):
        t.matmul(T["v%d" % h][:, 0:PW], T["ls%d" % h][:], x(0), True, True).then_inc(S["pe%d" % h], 1)
    for q in range(1, N):
        for h in range(NP):
            t.wait_ge(S["ve%d" % h], q)
            if q < N - 1:
                t.matmul(T["v%d" % h][:, 0:PW], T.lrep[:], T["p%d" % h][:], True, True).then_inc(S["pe%d" % h], 1)
            else:
                t.matmul(T["v%d" % h][0:32, 0:PW], T.lfin[:], T["p%d" % h][:], True, True).then_inc(S["pe%d" % h], 1)

    for h in range(0, NP, 2):
        s.wait_ge(S["pe%d" % h], N)
        s.activation(T.ysb[:, h * PW:(h + 1) * PW], T["v%d" % h][0:32, 0:PW], COPY).then_inc(S["yc%d" % h], 1)

    for h in range(0, NP, 2):
        g.sync.wait_ge(S["yc%d" % h], 1)
        g.sync.wait_ge(S["yc%d" % (h + 1)], 1)
        g.sync.dma_start(T.y[:, h * PW:(h + 2) * PW], T.ysb[:, h * PW:(h + 2) * PW]).then_inc(S.st, 16)
    g.sync.wait_ge(S.st, 16 * (NP // 2))
